import numpy as np
import ml_dtypes


def mxq(x, axis, fmt="e4m3"):
    dtype, down = {"e4m3": (ml_dtypes.float8_e4m3fn, 7), "e5m2": (ml_dtypes.float8_e5m2, 14)}[fmt]
    v = np.moveaxis(np.asarray(x, np.float32).astype(ml_dtypes.bfloat16).astype(np.float64), axis, -1)
    blocks = v.reshape(v.shape[:-1] + (-1, 32))
    amax = np.abs(blocks).max(-1, keepdims=True)
    byte = np.maximum(np.where(amax > 0, np.frexp(amax)[1] - 1 + 127, 0) - down, 1)
    scale = np.exp2(byte - 127.0)
    codes = (blocks / scale).astype(np.float32).astype(dtype).astype(np.float64)
    return np.moveaxis((codes * scale).reshape(v.shape), -1, axis)


WIDE = False


def mx_kscale(k):
    if not WIDE:
        return np.ones(k)
    levels = np.array([10, -10, 5, -5, 0])
    if k % 512:
        return np.exp2(np.random.permutation(np.resize(levels, k // 32))).repeat(32)
    a = np.empty((k // 512, 16))
    for p in range(k // 512):
        a[p, :8] = np.random.permutation(np.resize(levels, 8))
        for g in range(8):
            far = levels[np.abs(levels - a[p, g]) >= 10]
            a[p, g + 8] = far[np.random.randint(len(far))]
    return np.exp2(a.ravel()).repeat(32)


def f64(x):
    return np.asarray(x).astype(np.float64)


def striped(idx):
    return np.tile(idx.reshape(-1, 16).T, (8, 1)).astype(np.uint16)


def unstriped(offs):
    return offs[:16].T.reshape(-1).astype(np.int64)


E2M1 = np.array([0.0, 0.5, 1.0, 1.5, 2.0, 3.0, 4.0, 6.0, -0.0, -0.5, -1.0, -1.5, -2.0, -3.0, -4.0, -6.0])


def pack_weight(w, fmt):
    k, n = w.shape
    w = f64(np.asarray(w, np.float32).astype(ml_dtypes.bfloat16)).reshape(k // 32, 32, n)
    amax = np.abs(w).max(1)
    if fmt == "e4m3":
        byte = np.frexp(amax)[1] - 1 + 127 - 7
    else:
        mant, ex = np.frexp(amax / 6.0)
        byte = np.where(mant > 0.5, ex, ex - 1) + 127
    byte = np.clip(np.where(amax > 0, byte, 1), 1, 254)
    scaled = (w * np.exp2(127.0 - byte)[:, None, :]).reshape(k, n).astype(np.float32)
    by_word = np.ascontiguousarray(scaled.reshape(k // 512, 128, 4, n).transpose(0, 1, 3, 2))
    if fmt == "e4m3":
        words = by_word.astype(ml_dtypes.float8_e4m3fn).view(np.uint8)
    else:
        c = by_word.astype(ml_dtypes.float4_e2m1fn).view(np.uint8) & 0xF
        words = (c[..., 0::2] | (c[..., 1::2] << 4)).reshape(k // 512, 128, 2 * n)
    return np.ascontiguousarray(words), np.ascontiguousarray(byte.astype(np.uint8).reshape(k // 512, 16, n))


def unpack_weight(words, scales, fmt):
    g, _, n = scales.shape
    words = np.ascontiguousarray(words).reshape(g, 128, n, -1)
    if fmt == "e4m3":
        vals = words.view(ml_dtypes.float8_e4m3fn).astype(np.float64)
    else:
        nib = np.empty((g, 128, n, 4), np.uint8)
        nib[..., 0::2] = words & 0xF
        nib[..., 1::2] = words >> 4
        vals = E2M1[nib]
    vals = vals * np.repeat(np.exp2(scales.astype(np.float64) - 127.0), 8, axis=1)[..., None]
    return vals.transpose(0, 1, 3, 2).reshape(g * 512, n)


def planes(y):
    n, m = y.shape
    v = y.astype(np.float32).astype(ml_dtypes.bfloat16).astype(np.float64).reshape(n // 32, 32, m)
    top = np.abs(v).max(1)
    byte = np.clip(np.where(top > 0, np.frexp(top)[1] - 1 + 127 - 7, 1), 1, 254)
    codes = (v * np.exp2(127.0 - byte)[:, None, :]).reshape(n, m).astype(np.float32).astype(ml_dtypes.float8_e4m3fn).view(np.uint8)
    words = codes.reshape(n // 512, 128, 4, m).transpose(0, 1, 3, 2)
    return np.ascontiguousarray(words), np.ascontiguousarray(byte.astype(np.uint8).reshape(n // 512, 16, m))


def gelu(v):
    return 0.5 * v * (1.0 + np.tanh(np.sqrt(2.0 / np.pi) * (v + 0.044715 * v**3)))


K, T, E, C, H, N = 512, 512, 2, 256, 512, 512


def by_expert(wq, xq):
    return np.concatenate([wq[e].T @ xq[:, e * C:(e + 1) * C] for e in range(E)], axis=1)


def setup_inputs():
    n = np.random.standard_normal
    s = mx_kscale(K)
    u = mx_kscale(H)
    slot_token = np.concatenate([np.random.permutation(T)[:C] for e in range(E)])
    partner = np.concatenate([np.random.permutation(T) for _ in range(-(-E * C // T))])[:E * C]
    x = pack_weight(n((K, T)) * s[:, None], "e4m3")
    wp = [pack_weight(m, "e2m1") for m in n((E, K, H)) / np.sqrt(K) / s[None, :, None] * u]
    return {
        "x_words": x[0],
        "x_scales": x[1],
        "w1": (n((E, K, H)) / np.sqrt(K) / s[None, :, None] * u).astype(np.float32),
        "wp_words": np.stack([m[0] for m in wp]),
        "wp_scales": np.stack([m[1] for m in wp]),
        "w2": (n((E, H, N)) / np.sqrt(H) / u[None, :, None]).astype(np.float32),
        "offs": striped(slot_token),
        "offs2": striped(partner),
    }


def reference(x_words, x_scales, w1, wp_words, wp_scales, w2, offs, offs2):
    w1q = mxq(f64(w1), 1, "e4m3")
    wp = np.stack([unpack_weight(wp_words[e], wp_scales[e], "e2m1") for e in range(E)])
    w2q = mxq(f64(w2), 1, "e4m3")
    idx, idx2 = unstriped(offs), unstriped(offs2)
    x = unpack_weight(x_words, x_scales, "e4m3")
    h = gelu(by_expert(w1q, x[:, idx]) + by_expert(wp, x[:, idx2]))
    y = by_expert(w2q, mxq(h, 0, "e4m3"))
    out = y
    out_0 = out
    return (out_0,) + planes(out_0)

@@ -1,0 +1,224 @@
+from contextlib import ExitStack
+
+import concourse.mybir as mybir
+
+K, T, E, C, H, N = 512, 512, 2, 256, 512, 512
+FLOPS = 2 * E * C * (2 * K * H + H * N)
+
+F32 = mybir.dt.float32
+BF16 = mybir.dt.bfloat16
+I32 = mybir.dt.int32
+U32 = mybir.dt.uint32
+U16 = mybir.dt.uint16
+U8 = mybir.dt.uint8
+FP8X4 = mybir.dt.float8_e4m3fn_x4
+FP4X4 = mybir.dt.float4_e2m1fn_x4
+GELU = mybir.ActivationFunctionType.Gelu_apprx_tanh
+
+P = 128
+PACK = 4
+BLK = 128
+HALF = 256
+
+
+def tile_moe_duo_s_gelu_kernel(
+    tc, x_words, x_scales, w1, wp_words, wp_scales, w2, offs, offs2, out_0, out_1, out_2
+):
+    nc = tc.nc
+    with ExitStack() as ctx:
+        keep = ctx.enter_context(tc.tile_pool(name="keep", bufs=1))
+        shared = ctx.enter_context(tc.tile_pool(name="shared", bufs=1))
+        psum = ctx.enter_context(tc.psum_pool(name="psum", bufs=1))
+
+        def sb(name, shape, dtype):
+            return keep.tile(shape, dtype, name=name, align_bytes=64)
+
+        lists = [keep.tile([P, E * C // 16], U16, name="offs_sb"), keep.tile([P, E * C // 16], U16, name="offs2_sb")]
+        xw = sb("xw", [P, T], U32)
+        xs = sb("xs", [P, T], U8)
+        wps_raw = sb("wps_raw", [P, E, H], U8)
+        wpw_raw = sb("wpw_raw", [P, E, 2 * H], U8)
+        warm = sb("warm", [P, 8], F32)
+        warm_out = sb("warm_out", [P, 8], F32)
+
+        nc.vector.memset(xs[:].bitcast(I32), 0)
+        nc.gpsimd.memset(warm[:], 0.0)
+        nc.gpsimd.memset(wps_raw[:].bitcast(I32), 0)
+        nc.scalar.activation(warm_out[:], warm[:], GELU)
+
+        raw = {}
+
+        def load_half(which, w, e, c):
+            tile = sb(f"raw_{which}{e}{c}", [P, PACK, HALF], F32)
+            nc.sync.dma_start(tile[:], w[e].rearrange("(p j) c -> p j c", j=PACK)[:, :, c * HALF:(c + 1) * HALF])
+            raw[which, e, c] = tile
+
+        nc.sync.dma_start(xw[:].bitcast(I32), x_words[0].rearrange("p t d -> p (t d)").bitcast(I32))
+        nc.sync.dma_start(lists[0][:], offs)
+        for q in range(4):
+            nc.sync.dma_start(xs[32 * q:32 * q + 4, :].bitcast(I32), x_scales[0, 4 * q:4 * q + 4, :].bitcast(I32))
+        load_half("a", w1, 0, 0)
+        load_half("a", w1, 0, 1)
+        nc.sync.dma_start(lists[1][:], offs2)
+        nc.sync.dma_start(wpw_raw[:].bitcast(I32), wp_words[:, 0].rearrange("e p c -> p e c").bitcast(I32))
+        for q in range(4):
+            nc.sync.dma_start(
+                wps_raw[32 * q:32 * q + 4, :, :].bitcast(I32),
+                wp_scales[:, 0, 4 * q:4 * q + 4, :].rearrange("e r c -> r e c").bitcast(I32),
+            )
+        for which, w, e in (("a", w1, 1), ("b", w2, 0), ("b", w2, 1)):
+            load_half(which, w, e, 0)
+            load_half(which, w, e, 1)
+
+        gw = {}
+        gs = {}
+
+        def gather(li, e):
+            ol = lists[li][:, e * C // 16:(e + 1) * C // 16]
+            if (li, e) == (1, 1):
+                gw[li, e] = shared.tile([P, C], U32, name="gw11", align_bytes=64, offset=0)
+                gs[li, e] = shared.tile([P, C], U8, name="gs11", align_bytes=64, offset=4 * C)
+            else:
+                gw[li, e] = sb(f"gw{li}{e}", [P, C], U32)
+                gs[li, e] = sb(f"gs{li}{e}", [P, C], U8)
+            nc.vector.tensor_copy(gw[li, e][:], xw[:].indirect(ol))
+            nc.vector.tensor_copy(gs[li, e][:], xs[:].indirect(ol))
+
+        wpw = sb("wpw", [P, E, 2 * H], U8)
+        wps = sb("wps", [P, E, H], U8)
+
+        def deal_wp(e):
+            nc.vector.tensor_copy(
+                wpw[:, e, :].bitcast(U16).rearrange("p (t b i) -> p b t i", t=PACK, i=8),
+                wpw_raw[:, e, :].bitcast(U16).rearrange("p (b i t) -> p b t i", t=PACK, i=8),
+            )
+            nc.vector.tensor_copy(
+                wps[:, e, :].rearrange("p (t b i) -> p b t i", t=PACK, i=16),
+                wps_raw[:, e, :].rearrange("p (b i t) -> p b t i", t=PACK, i=16),
+            )
+
+        grouped = {}
+        codes = {}
+        scales = {}
+
+        def cast(which, e, c, m0, m1, copy):
+            if (which, e, c) == ("a", 0, 0):
+                grouped[which, e] = shared.tile([P, PACK, P, PACK], BF16, name="grp_a0", align_bytes=64, offset=0)
+            elif (which, e) not in grouped:
+                grouped[which, e] = sb(f"grp_{which}{e}", [P, PACK, P, PACK], BF16)
+            base = c * HALF // PACK
+            copy(
+                grouped[which, e][:, :, base + m0:base + m1, :].rearrange("p t m j -> p m j t"),
+                raw[which, e, c][:].rearrange("p j (m t) -> p m j t", t=PACK)[:, m0:m1],
+            )
+
+        def quant_w(which, e, pieces):
+            codes[which, e] = sb(f"codes_{which}{e}", [P, H], U32)
+            scales[which, e] = sb(f"scales_{which}{e}", [P, H], U8)
+            flat = grouped[which, e][:].rearrange("p t m j -> p (t m j)")
+            w = H // pieces
+            for i in range(pieces):
+                nc.vector.quantize_mx(
+                    out=codes[which, e][:, i * w:(i + 1) * w].bitcast(FP8X4),
+                    scales=scales[which, e][:, i * w:(i + 1) * w],
+                    in_=flat[:, PACK * i * w:PACK * (i + 1) * w],
+                )
+
+        hc = {}
+        hs = {}
+
+        def layer1(e):
+            for b in range(C // BLK):
+                cols = slice(b * BLK, (b + 1) * BLK)
+                acc = psum.tile([P, PACK, BLK], F32, name=f"acc1_{e}{b}")
+                for t in range(PACK):
+                    nc.tensor.matmul_mx(
+                        out=acc[:, t, :],
+                        lhsT=wpw[:, e, 2 * P * t:2 * P * (t + 1)].bitcast(FP4X4),
+                        lhsT_scale=wps[:, e, P * t:P * (t + 1)],
+                        rhs=gw[1, e][:, cols].bitcast(FP8X4),
+                        rhs_scale=gs[1, e][:, cols],
+                        start=True,
+                        stop=False,
+                    )
+                    nc.tensor.matmul_mx(
+                        out=acc[:, t, :],
+                        lhsT=codes["a", e][:, P * t:P * (t + 1)].bitcast(FP8X4),
+                        lhsT_scale=scales["a", e][:, P * t:P * (t + 1)],
+                        rhs=gw[0, e][:, cols].bitcast(FP8X4),
+                        rhs_scale=gs[0, e][:, cols],
+                        start=False,
+                        stop=True,
+                    )
+                hb = sb(f"hb{e}{b}", [P, BLK, PACK], BF16)
+                nc.scalar.activation(hb[:], acc[:].rearrange("p t s -> p s t"), GELU)
+                hc[e, b] = sb(f"hc{e}{b}", [P, BLK], U32)
+                hs[e, b] = sb(f"hs{e}{b}", [P, BLK], U8)
+                nc.vector.quantize_mx(
+                    out=hc[e, b][:].bitcast(FP8X4), scales=hs[e, b][:], in_=hb[:].rearrange("p s t -> p (s t)")
+                )
+
+        yc = sb("yc", [P, E * C], U32)
+        ysc = sb("ysc", [P, E * C], U8)
+        out_rows = out_0.rearrange("(p t) s -> p t s", t=PACK)
+        out_words = out_1[0].rearrange("p s d -> p (s d)").bitcast(I32)
+
+        def layer2(e):
+            y = sb(f"y{e}", [P, PACK, C], F32)
+            for b in range(C // BLK):
+                cols = slice(b * BLK, (b + 1) * BLK)
+                acc = psum.tile([P, PACK, BLK], F32, name=f"acc2_{e}{b}")
+                for t in range(PACK):
+                    nc.tensor.matmul_mx(
+                        out=acc[:, t, :],
+                        lhsT=codes["b", e][:, P * t:P * (t + 1)].bitcast(FP8X4),
+                        lhsT_scale=scales["b", e][:, P * t:P * (t + 1)],
+                        rhs=hc[e, b][:].bitcast(FP8X4),
+                        rhs_scale=hs[e, b][:],
+                        start=True,
+                        stop=True,
+                    )
+                nc.scalar.copy(y[:, :, cols], acc[:])
+                yb = sb(f"yb{e}{b}", [P, BLK, PACK], BF16)
+                nc.vector.tensor_copy(
+                    yb[:].rearrange("p (c i) t -> p c t i", i=4),
+                    y[:, :, cols].rearrange("p t (c i) -> p c t i", i=4),
+                )
+                g = slice(e * C + b * BLK, e * C + (b + 1) * BLK)
+                nc.vector.quantize_mx(
+                    out=yc[:, g].bitcast(FP8X4), scales=ysc[:, g], in_=yb[:].rearrange("p s t -> p (s t)")
+                )
+            ecols = slice(e * C, (e + 1) * C)
+            nc.sync.dma_start(out_rows[:, :, ecols], y[:])
+            nc.sync.dma_start(out_words[:, ecols], yc[:, ecols].bitcast(I32))
+
+        s_copy = nc.scalar.copy
+        v_copy = nc.vector.tensor_copy
+        M = HALF // PACK
+
+        gather(0, 0)
+        gather(0, 1)
+        gather(1, 0)
+        cast("a", 0, 0, 0, M, s_copy)
+        cast("a", 0, 1, 0, M, s_copy)
+        deal_wp(0)
+        quant_w("a", 0, 2)
+        gather(1, 1)
+        deal_wp(1)
+        cast("a", 1, 0, 0, M, s_copy)
+        cast("a", 1, 1, 0, M, s_copy)
+        layer1(0)
+        quant_w("a", 1, 2)
+        cast("b", 0, 0, 0, M, v_copy)
+        cast("b", 0, 1, 0, M, s_copy)
+        layer1(1)
+        quant_w("b", 0, 2)
+        cast("b", 1, 0, 0, M, v_copy)
+        cast("b", 1, 1, 0, 44, v_copy)
+        cast("b", 1, 1, 44, M, s_copy)
+        layer2(0)
+        quant_w("b", 1, 4)
+        layer2(1)
+        for q in range(4):
+            eng = nc.sync if q % 2 == 0 else nc.scalar
+            eng.dma_start(out_2[0, 4 * q:4 * q + 4, :].bitcast(I32), ysc[32 * q:32 * q + 4, :].bitcast(I32))

@@ -36,62 +36,72 @@ def tile_moe_duo_s_gelu_kernel(
         lists = [keep.tile([P, E * C // 16], U16, name="offs_sb"), keep.tile([P, E * C // 16], U16, name="offs2_sb")]
         xw = sb("xw", [P, T], U32)
         xs = sb("xs", [P, T], U8)
-        wps_raw = sb("wps_raw", [P, E, H], U8)
+        wps_raw = shared.tile([P, E, H], U8, name="wps_raw", align_bytes=64, offset=4096)
         wpw_raw = sb("wpw_raw", [P, E, 2 * H], U8)
         warm = sb("warm", [P, 8], F32)
         warm_out = sb("warm_out", [P, 8], F32)
 
         nc.vector.memset(xs[:].bitcast(I32), 0)
+        nc.vector.memset(wps_raw[:].bitcast(I32), 0)
         nc.gpsimd.memset(warm[:], 0.0)
-        nc.gpsimd.memset(wps_raw[:].bitcast(I32), 0)
         nc.scalar.activation(warm_out[:], warm[:], GELU)
 
         raw = {}
 
         def load_half(which, w, e, c):
-            tile = sb(f"raw_{which}{e}{c}", [P, PACK, HALF], F32)
+            if (which, e, c) == ("b", 0, 0):
+                tile = shared.tile([P, PACK, HALF], F32, name="raw_b00", align_bytes=64, offset=0)
+            else:
+                tile = sb(f"raw_{which}{e}{c}", [P, PACK, HALF], F32)
             nc.sync.dma_start(tile[:], w[e].rearrange("(p j) c -> p j c", j=PACK)[:, :, c * HALF:(c + 1) * HALF])
             raw[which, e, c] = tile
 
         nc.sync.dma_start(xw[:].bitcast(I32), x_words[0].rearrange("p t d -> p (t d)").bitcast(I32))
         nc.sync.dma_start(lists[0][:], offs)
+        load_half("a", w1, 0, 0)
         for q in range(4):
             nc.sync.dma_start(xs[32 * q:32 * q + 4, :].bitcast(I32), x_scales[0, 4 * q:4 * q + 4, :].bitcast(I32))
-        load_half("a", w1, 0, 0)
         load_half("a", w1, 0, 1)
         nc.sync.dma_start(lists[1][:], offs2)
         nc.sync.dma_start(wpw_raw[:].bitcast(I32), wp_words[:, 0].rearrange("e p c -> p e c").bitcast(I32))
+        load_half("a", w1, 1, 0)
         for q in range(4):
             nc.sync.dma_start(
                 wps_raw[32 * q:32 * q + 4, :, :].bitcast(I32),
                 wp_scales[:, 0, 4 * q:4 * q + 4, :].rearrange("e r c -> r e c").bitcast(I32),
             )
-        for which, w, e in (("a", w1, 1), ("b", w2, 0), ("b", w2, 1)):
-            load_half(which, w, e, 0)
-            load_half(which, w, e, 1)
+        load_half("a", w1, 1, 1)
+        for e in range(E):
+            load_half("b", w2, e, 0)
+            load_half("b", w2, e, 1)
 
         gw = {}
         gs = {}
 
-        def gather(li, e):
-            ol = lists[li][:, e * C // 16:(e + 1) * C // 16]
+        def gather_words(li, e):
             if (li, e) == (1, 1):
-                gw[li, e] = shared.tile([P, C], U32, name="gw11", align_bytes=64, offset=0)
-                gs[li, e] = shared.tile([P, C], U8, name="gs11", align_bytes=64, offset=4 * C)
+                gw[li, e] = shared.tile([P, C], U32, name="gw11", align_bytes=64, offset=4096 + C)
             else:
                 gw[li, e] = sb(f"gw{li}{e}", [P, C], U32)
+            nc.vector.tensor_copy(gw[li, e][:], xw[:].indirect(lists[li][:, e * C // 16:(e + 1) * C // 16]))
+
+        def gather_scales(li, e):
+            if (li, e) == (1, 1):
+                gs[li, e] = shared.tile([P, C], U8, name=f"gs{li}{e}", align_bytes=64, offset=4096)
+            else:
                 gs[li, e] = sb(f"gs{li}{e}", [P, C], U8)
-            nc.vector.tensor_copy(gw[li, e][:], xw[:].indirect(ol))
-            nc.vector.tensor_copy(gs[li, e][:], xs[:].indirect(ol))
+            nc.vector.tensor_copy(gs[li, e][:], xs[:].indirect(lists[li][:, e * C // 16:(e + 1) * C // 16]))
 
         wpw = sb("wpw", [P, E, 2 * H], U8)
         wps = sb("wps", [P, E, H], U8)
 
-        def deal_wp(e):
+        def deal_words():
             nc.vector.tensor_copy(
-                wpw[:, e, :].bitcast(U16).rearrange("p (t b i) -> p b t i", t=PACK, i=8),
-                wpw_raw[:, e, :].bitcast(U16).rearrange("p (b i t) -> p b t i", t=PACK, i=8),
+                wpw[:].bitcast(U16).rearrange("p e (t b i) -> p e b t i", t=PACK, i=8),
+                wpw_raw[:].bitcast(U16).rearrange("p e (b i t) -> p e b t i", t=PACK, i=8),
             )
+
+        def deal_scales(e):
             nc.vector.tensor_copy(
                 wps[:, e, :].rearrange("p (t b i) -> p b t i", t=PACK, i=16),
                 wps_raw[:, e, :].rearrange("p (b i t) -> p b t i", t=PACK, i=16),
@@ -102,9 +112,7 @@ def tile_moe_duo_s_gelu_kernel(
         scales = {}
 
         def cast(which, e, c, m0, m1, copy):
-            if (which, e, c) == ("a", 0, 0):
-                grouped[which, e] = shared.tile([P, PACK, P, PACK], BF16, name="grp_a0", align_bytes=64, offset=0)
-            elif (which, e) not in grouped:
+            if (which, e) not in grouped:
                 grouped[which, e] = sb(f"grp_{which}{e}", [P, PACK, P, PACK], BF16)
             base = c * HALF // PACK
             copy(
@@ -150,7 +158,7 @@ def tile_moe_duo_s_gelu_kernel(
                         start=False,
                         stop=True,
                     )
-                hb = sb(f"hb{e}{b}", [P, BLK, PACK], BF16)
+                hb = shared.tile([P, BLK, PACK], BF16, name=f"hb{e}{b}", align_bytes=64, offset=1024 * (2 * e + b))
                 nc.scalar.activation(hb[:], acc[:].rearrange("p t s -> p s t"), GELU)
                 hc[e, b] = sb(f"hc{e}{b}", [P, BLK], U32)
                 hs[e, b] = sb(f"hs{e}{b}", [P, BLK], U8)
@@ -196,28 +204,32 @@ def tile_moe_duo_s_gelu_kernel(
         v_copy = nc.vector.tensor_copy
         M = HALF // PACK
 
-        gather(0, 0)
-        gather(0, 1)
-        gather(1, 0)
+        for e in range(E):
+            gather_words(0, e)
+        for e in range(E):
+            gather_scales(0, e)
+        gather_words(1, 0)
+        gather_scales(1, 0)
+        deal_words()
         cast("a", 0, 0, 0, M, s_copy)
         cast("a", 0, 1, 0, M, s_copy)
-        deal_wp(0)
-        quant_w("a", 0, 2)
-        gather(1, 1)
-        deal_wp(1)
+        quant_w("a", 0, 1)
+        deal_scales(0)
+        deal_scales(1)
+        gather_words(1, 1)
+        gather_scales(1, 1)
         cast("a", 1, 0, 0, M, s_copy)
         cast("a", 1, 1, 0, M, s_copy)
-        layer1(0)
-        quant_w("a", 1, 2)
-        cast("b", 0, 0, 0, M, v_copy)
-        cast("b", 0, 1, 0, M, s_copy)
-        layer1(1)
-        quant_w("b", 0, 2)
+        quant_w("a", 1, 1)
+        cast("b", 0, 0, 0, M, s_copy)
+        cast("b", 0, 1, 0, M, v_copy)
+        quant_w("b", 0, 1)
         cast("b", 1, 0, 0, M, v_copy)
-        cast("b", 1, 1, 0, 44, v_copy)
-        cast("b", 1, 1, 44, M, s_copy)
+        cast("b", 1, 1, 0, M, v_copy)
+        quant_w("b", 1, 2)
+        layer1(0)
+        layer1(1)
         layer2(0)
-        quant_w("b", 1, 4)
         layer2(1)
         for q in range(4):
             eng = nc.sync if q % 2 == 0 else nc.scalar

@@ -38,23 +38,26 @@ def tile_moe_duo_s_gelu_kernel(
         xs = sb("xs", [P, T], U8)
         wps_raw = shared.tile([P, E, H], U8, name="wps_raw", align_bytes=64, offset=4096)
         wpw_raw = sb("wpw_raw", [P, E, 2 * H], U8)
+
         warm = sb("warm", [P, 8], F32)
         warm_out = sb("warm_out", [P, 8], F32)
-
-        nc.vector.memset(xs[:].bitcast(I32), 0)
-        nc.vector.memset(wps_raw[:].bitcast(I32), 0)
         nc.gpsimd.memset(warm[:], 0.0)
         nc.scalar.activation(warm_out[:], warm[:], GELU)
+        nc.vector.memset(xs[:].bitcast(I32), 0)
+        nc.vector.memset(wps_raw[:].bitcast(I32), 0)
 
         raw = {}
+        first = {}
 
-        def load_half(which, w, e, c):
+        def load_half(which, w, e, c, c0=None, width=HALF):
+            c0 = c * HALF if c0 is None else c0
             if (which, e, c) == ("b", 0, 0):
-                tile = shared.tile([P, PACK, HALF], F32, name="raw_b00", align_bytes=64, offset=0)
+                tile = shared.tile([P, PACK, width], F32, name="raw_b00", align_bytes=64, offset=0)
             else:
-                tile = sb(f"raw_{which}{e}{c}", [P, PACK, HALF], F32)
-            nc.sync.dma_start(tile[:], w[e].rearrange("(p j) c -> p j c", j=PACK)[:, :, c * HALF:(c + 1) * HALF])
+                tile = sb(f"raw_{which}{e}{c}", [P, PACK, width], F32)
+            nc.sync.dma_start(tile[:], w[e].rearrange("(p j) c -> p j c", j=PACK)[:, :, c0:c0 + width])
             raw[which, e, c] = tile
+            first[which, e, c] = c0 // PACK
 
         nc.sync.dma_start(xw[:].bitcast(I32), x_words[0].rearrange("p t d -> p (t d)").bitcast(I32))
         nc.sync.dma_start(lists[0][:], offs)
@@ -71,9 +74,11 @@ def tile_moe_duo_s_gelu_kernel(
                 wp_scales[:, 0, 4 * q:4 * q + 4, :].rearrange("e r c -> r e c").bitcast(I32),
             )
         load_half("a", w1, 1, 1)
-        for e in range(E):
-            load_half("b", w2, e, 0)
-            load_half("b", w2, e, 1)
+        load_half("b", w2, 0, 0)
+        load_half("b", w2, 0, 1)
+        load_half("b", w2, 1, 0)
+        load_half("b", w2, 1, 1, 256, 128)
+        load_half("b", w2, 1, 2, 384, 128)
 
         gw = {}
         gs = {}
@@ -114,7 +119,7 @@ def tile_moe_duo_s_gelu_kernel(
         def cast(which, e, c, m0, m1, copy):
             if (which, e) not in grouped:
                 grouped[which, e] = sb(f"grp_{which}{e}", [P, PACK, P, PACK], BF16)
-            base = c * HALF // PACK
+            base = first[which, e, c]
             copy(
                 grouped[which, e][:, :, base + m0:base + m1, :].rearrange("p t m j -> p m j t"),
                 raw[which, e, c][:].rearrange("p j (m t) -> p m j t", t=PACK)[:, m0:m1],
@@ -172,7 +177,6 @@ def tile_moe_duo_s_gelu_kernel(
         out_words = out_1[0].rearrange("p s d -> p (s d)").bitcast(I32)
 
         def layer2(e):
-            y = sb(f"y{e}", [P, PACK, C], F32)
             for b in range(C // BLK):
                 cols = slice(b * BLK, (b + 1) * BLK)
                 acc = psum.tile([P, PACK, BLK], F32, name=f"acc2_{e}{b}")
@@ -186,18 +190,25 @@ def tile_moe_duo_s_gelu_kernel(
                         start=True,
                         stop=True,
                     )
-                nc.scalar.copy(y[:, :, cols], acc[:])
-                yb = sb(f"yb{e}{b}", [P, BLK, PACK], BF16)
-                nc.vector.tensor_copy(
-                    yb[:].rearrange("p (c i) t -> p c t i", i=4),
-                    y[:, :, cols].rearrange("p t (c i) -> p c t i", i=4),
-                )
                 g = slice(e * C + b * BLK, e * C + (b + 1) * BLK)
+                y = sb(f"y{e}{b}", [P, PACK, BLK], F32)
+                if (e, b) == (1, 0):
+                    nc.vector.tensor_copy(y[:], acc[:])
+                else:
+                    nc.scalar.copy(y[:], acc[:])
+                nc.sync.dma_start(out_rows[:, :, g], y[:])
+                yb = sb(f"yb{e}{b}", [P, BLK, PACK], BF16)
+                if e == 0:
+                    nc.scalar.copy(yb[:], acc[:].rearrange("p t s -> p s t"))
+                else:
+                    nc.vector.tensor_copy(
+                        yb[:].rearrange("p (c i) t -> p c t i", i=4),
+                        y[:].rearrange("p t (c i) -> p c t i", i=4),
+                    )
                 nc.vector.quantize_mx(
                     out=yc[:, g].bitcast(FP8X4), scales=ysc[:, g], in_=yb[:].rearrange("p s t -> p (s t)")
                 )
             ecols = slice(e * C, (e + 1) * C)
-            nc.sync.dma_start(out_rows[:, :, ecols], y[:])
             nc.sync.dma_start(out_words[:, ecols], yc[:, ecols].bitcast(I32))
 
         s_copy = nc.scalar.copy
@@ -224,10 +235,11 @@ def tile_moe_duo_s_gelu_kernel(
         cast("b", 0, 0, 0, M, s_copy)
         cast("b", 0, 1, 0, M, v_copy)
         quant_w("b", 0, 1)
-        cast("b", 1, 0, 0, M, v_copy)
-        cast("b", 1, 1, 0, M, v_copy)
-        quant_w("b", 1, 2)
         layer1(0)
+        cast("b", 1, 0, 0, M, v_copy)
+        cast("b", 1, 1, 0, M // 2, v_copy)
+        cast("b", 1, 2, 0, M // 2, v_copy)
+        quant_w("b", 1, 2)
         layer1(1)
         layer2(0)
         layer2(1)

@@ -18,7 +18,7 @@ GELU = mybir.ActivationFunctionType.Gelu_apprx_tanh
 P = 128
 PACK = 4
 BLK = 128
-HALF = 256
+WIN = 704
 
 
 def tile_moe_duo_s_gelu_kernel(
@@ -30,219 +30,274 @@ def tile_moe_duo_s_gelu_kernel(
         shared = ctx.enter_context(tc.tile_pool(name="shared", bufs=1))
         psum = ctx.enter_context(tc.psum_pool(name="psum", bufs=1))
 
+        offsets = {
+            "raw_b0": 0, "hb1": 0,
+            "raw_b11": 12288, "hc1": 12288, "hs1": 13312, "yb00": 14336, "yb01": 15360,
+            "codes_b11": 8192, "ysc": 8192,
+            "raw_a1": 24576, "hb0": 24576, "gs11": 28672,
+            "wpw_raw": 34816, "scales_a00": 34816, "scales_a01": 35840,
+        }
+
         def sb(name, shape, dtype):
+            if name in offsets:
+                return shared.tile(shape, dtype, name=name, align_bytes=64, offset=offsets[name])
             return keep.tile(shape, dtype, name=name, align_bytes=64)
 
         lists = [keep.tile([P, E * C // 16], U16, name="offs_sb"), keep.tile([P, E * C // 16], U16, name="offs2_sb")]
-        xw = sb("xw", [P, T], U32)
-        xs = sb("xs", [P, T], U8)
-        wps_raw = shared.tile([P, E, H], U8, name="wps_raw", align_bytes=64, offset=4096)
+        xw = sb("xw", [P, WIN], U32)
+        xs = sb("xs", [P, WIN], U8)
+        wps_raw = sb("wps_raw", [P, E, H], U8)
         wpw_raw = sb("wpw_raw", [P, E, 2 * H], U8)
-
         warm = sb("warm", [P, 8], F32)
         warm_out = sb("warm_out", [P, 8], F32)
+        nc.gpsimd.memset(xs[:].bitcast(I32), 0)
         nc.gpsimd.memset(warm[:], 0.0)
-        nc.scalar.activation(warm_out[:], warm[:], GELU)
-        nc.vector.memset(xs[:].bitcast(I32), 0)
+        nc.vector.memset(xw[:, T:].bitcast(I32), 0)
         nc.vector.memset(wps_raw[:].bitcast(I32), 0)
 
         raw = {}
-        first = {}
+        for which, e in (("a", 0), ("a", 1), ("b", 0)):
+            raw[which, e] = sb(f"raw_{which}{e}", [P, PACK, H], F32)
+        last = [sb(f"raw_b1{c}", [P, PACK, N // 2], F32) for c in range(2)]
 
-        def load_half(which, w, e, c, c0=None, width=HALF):
-            c0 = c * HALF if c0 is None else c0
-            if (which, e, c) == ("b", 0, 0):
-                tile = shared.tile([P, PACK, width], F32, name="raw_b00", align_bytes=64, offset=0)
-            else:
-                tile = sb(f"raw_{which}{e}{c}", [P, PACK, width], F32)
-            nc.sync.dma_start(tile[:], w[e].rearrange("(p j) c -> p j c", j=PACK)[:, :, c0:c0 + width])
-            raw[which, e, c] = tile
-            first[which, e, c] = c0 // PACK
+        def load_w1(e):
+            nc.sync.dma_start(raw["a", e][:], w1[e].rearrange("(p j) c -> p j c", j=PACK))
 
-        nc.sync.dma_start(xw[:].bitcast(I32), x_words[0].rearrange("p t d -> p (t d)").bitcast(I32))
+        def load_w2(e, tile, c0, c1):
+            rows = w2[e].rearrange("(q j r) c -> r q j c", j=PACK, r=2)
+            for r in range(2):
+                nc.sync.dma_start(tile[r:P:2], rows[r][:, :, c0:c1])
+
+        nc.sync.dma_start(xw[:, :T].bitcast(I32), x_words[0].rearrange("p t d -> p (t d)").bitcast(I32))
         nc.sync.dma_start(lists[0][:], offs)
-        load_half("a", w1, 0, 0)
         for q in range(4):
-            nc.sync.dma_start(xs[32 * q:32 * q + 4, :].bitcast(I32), x_scales[0, 4 * q:4 * q + 4, :].bitcast(I32))
-        load_half("a", w1, 0, 1)
+            eng = nc.scalar if q < 2 else nc.sync
+            eng.dma_start(xs[32 * q:32 * q + 4, :T].bitcast(I32), x_scales[0, 4 * q:4 * q + 4, :].bitcast(I32))
         nc.sync.dma_start(lists[1][:], offs2)
-        nc.sync.dma_start(wpw_raw[:].bitcast(I32), wp_words[:, 0].rearrange("e p c -> p e c").bitcast(I32))
-        load_half("a", w1, 1, 0)
+        load_w1(0)
         for q in range(4):
             nc.sync.dma_start(
                 wps_raw[32 * q:32 * q + 4, :, :].bitcast(I32),
                 wp_scales[:, 0, 4 * q:4 * q + 4, :].rearrange("e r c -> r e c").bitcast(I32),
             )
-        load_half("a", w1, 1, 1)
-        load_half("b", w2, 0, 0)
-        load_half("b", w2, 0, 1)
-        load_half("b", w2, 1, 0)
-        load_half("b", w2, 1, 1, 256, 128)
-        load_half("b", w2, 1, 2, 384, 128)
+        nc.sync.dma_start(wpw_raw[:].bitcast(I32), wp_words[:, 0].rearrange("e p c -> p e c").bitcast(I32))
+        load_w1(1)
+        load_w2(0, raw["b", 0], 0, N)
+        for c in range(2):
+            load_w2(1, last[c], c * N // 2, (c + 1) * N // 2)
+        nc.scalar.activation(warm_out[:], warm[:], GELU)
 
-        gw = {}
-        gs = {}
+        gw = [sb(f"gw{li}", [P, E * C], U32) for li in range(2)]
+        gs0 = sb("gs0", [P, E * C], U8)
+        gs = {(0, e): gs0[:, e * C:(e + 1) * C] for e in range(E)}
+        for e in range(E):
+            gs[1, e] = sb(f"gs1{e}", [P, C], U8)[:]
 
-        def gather_words(li, e):
-            if (li, e) == (1, 1):
-                gw[li, e] = shared.tile([P, C], U32, name="gw11", align_bytes=64, offset=4096 + C)
-            else:
-                gw[li, e] = sb(f"gw{li}{e}", [P, C], U32)
-            nc.vector.tensor_copy(gw[li, e][:], xw[:].indirect(lists[li][:, e * C // 16:(e + 1) * C // 16]))
+        def gather_words(li, s0, s1):
+            nc.vector.tensor_copy(gw[li][:, s0:s1], xw[:].indirect(lists[li][:, s0 // 16:s1 // 16]))
 
-        def gather_scales(li, e):
-            if (li, e) == (1, 1):
-                gs[li, e] = shared.tile([P, C], U8, name=f"gs{li}{e}", align_bytes=64, offset=4096)
-            else:
-                gs[li, e] = sb(f"gs{li}{e}", [P, C], U8)
-            nc.vector.tensor_copy(gs[li, e][:], xs[:].indirect(lists[li][:, e * C // 16:(e + 1) * C // 16]))
+        def gather_scales(out, li, s0, s1):
+            nc.vector.tensor_copy(out, xs[:].indirect(lists[li][:, s0 // 16:s1 // 16]))
 
         wpw = sb("wpw", [P, E, 2 * H], U8)
         wps = sb("wps", [P, E, H], U8)
 
         def deal_words():
             nc.vector.tensor_copy(
-                wpw[:].bitcast(U16).rearrange("p e (t b i) -> p e b t i", t=PACK, i=8),
-                wpw_raw[:].bitcast(U16).rearrange("p e (b i t) -> p e b t i", t=PACK, i=8),
+                wpw[:].bitcast(I32).rearrange("p e (t b i) -> p e b t i", t=PACK, i=4),
+                wpw_raw[:].bitcast(I32).rearrange("p e (b i t) -> p e b t i", t=PACK, i=4),
             )
 
-        def deal_scales(e):
+        def deal_scales():
             nc.vector.tensor_copy(
-                wps[:, e, :].rearrange("p (t b i) -> p b t i", t=PACK, i=16),
-                wps_raw[:, e, :].rearrange("p (b i t) -> p b t i", t=PACK, i=16),
+                wps[:].bitcast(U16).rearrange("p e (t b i) -> p e b t i", t=PACK, i=8),
+                wps_raw[:].bitcast(U16).rearrange("p e (b i t) -> p e b t i", t=PACK, i=8),
             )
 
         grouped = {}
         codes = {}
         scales = {}
-
-        def cast(which, e, c, m0, m1, copy):
-            if (which, e) not in grouped:
+        for which in "ab":
+            for e in range(E):
                 grouped[which, e] = sb(f"grp_{which}{e}", [P, PACK, P, PACK], BF16)
-            base = first[which, e, c]
+                for u in range(2):
+                    pair_codes = sb(f"codes_{which}{e}{u}", [P, 2 * P], U32)
+                    pair_scales = sb(f"scales_{which}{e}{u}", [P, 2 * P], U8)
+                    codes[which, e, u] = pair_codes
+                    scales[which, e, u] = pair_scales
+
+        def cast_w1(e, t0, t1, copy):
             copy(
-                grouped[which, e][:, :, base + m0:base + m1, :].rearrange("p t m j -> p m j t"),
-                raw[which, e, c][:].rearrange("p j (m t) -> p m j t", t=PACK)[:, m0:m1],
+                grouped["a", e][:, t0:t1].rearrange("p t (q r) j -> p q j t r", r=2),
+                raw["a", e][:].rearrange("p j (q t r) -> p q j t r", t=PACK, r=2)[:, :, :, t0:t1, :],
             )
 
-        def quant_w(which, e, pieces):
-            codes[which, e] = sb(f"codes_{which}{e}", [P, H], U32)
-            scales[which, e] = sb(f"scales_{which}{e}", [P, H], U8)
-            flat = grouped[which, e][:].rearrange("p t m j -> p (t m j)")
-            w = H // pieces
-            for i in range(pieces):
-                nc.vector.quantize_mx(
-                    out=codes[which, e][:, i * w:(i + 1) * w].bitcast(FP8X4),
-                    scales=scales[which, e][:, i * w:(i + 1) * w],
-                    in_=flat[:, PACK * i * w:PACK * (i + 1) * w],
+        def cast_w2(e, t0, t1, copy):
+            copy(
+                grouped["b", e][:, t0:t1].rearrange("p t m j -> p m j t"),
+                raw["b", e][:].rearrange("p j (m t) -> p m j t", t=PACK)[:, :, :, t0:t1],
+            )
+
+        def cast_last(c, t0, t1, copy):
+            copy(
+                grouped["b", 1][:, t0:t1, c * P // 2:(c + 1) * P // 2].rearrange("p t m j -> p m j t"),
+                last[c][:].rearrange("p j (m t) -> p m j t", t=PACK)[:, :, :, t0:t1],
+            )
+
+        def quant_w(which, e, t0, t1):
+            nc.vector.quantize_mx(
+                out=codes[which, e, t0 // 2][:, P * (t0 % 2):P * (t1 - t0 + t0 % 2)].bitcast(FP8X4),
+                scales=scales[which, e, t0 // 2][:, P * (t0 % 2):P * (t1 - t0 + t0 % 2)],
+                in_=grouped[which, e][:, t0:t1].rearrange("p t m j -> p (t m j)"),
+            )
+
+        hb = [sb(f"hb{e}", [P, C, PACK], BF16) for e in range(E)]
+        hc = [sb(f"hc{e}", [P, C], U32) for e in range(E)]
+        hs = [sb(f"hs{e}", [P, C], U8) for e in range(E)]
+        acc1 = {}
+
+        def layer1(e, b):
+            cols = slice(e * C + b * BLK, e * C + (b + 1) * BLK)
+            acc = psum.tile([P, PACK, BLK], F32, name=f"acc1_{e}{b}")
+            acc1[e, b] = acc
+            for t in range(PACK):
+                nc.tensor.matmul_mx(
+                    out=acc[:, t, :],
+                    lhsT=wpw[:, e, 2 * P * t:2 * P * (t + 1)].bitcast(FP4X4),
+                    lhsT_scale=wps[:, e, P * t:P * (t + 1)],
+                    rhs=gw[1][:, cols].bitcast(FP8X4),
+                    rhs_scale=gs[1, e][:, b * BLK:(b + 1) * BLK],
+                    start=True,
+                    stop=False,
+                )
+                nc.tensor.matmul_mx(
+                    out=acc[:, t, :],
+                    lhsT=codes["a", e, t // 2][:, P * (t % 2):P * (t % 2 + 1)].bitcast(FP8X4),
+                    lhsT_scale=scales["a", e, t // 2][:, P * (t % 2):P * (t % 2 + 1)],
+                    rhs=gw[0][:, cols].bitcast(FP8X4),
+                    rhs_scale=gs[0, e][:, b * BLK:(b + 1) * BLK],
+                    start=False,
+                    stop=True,
                 )
 
-        hc = {}
-        hs = {}
+        def gelu(e, b):
+            nc.scalar.activation(hb[e][:, b * BLK:(b + 1) * BLK, :], acc1[e, b][:].rearrange("p t s -> p s t"), GELU)
 
-        def layer1(e):
-            for b in range(C // BLK):
-                cols = slice(b * BLK, (b + 1) * BLK)
-                acc = psum.tile([P, PACK, BLK], F32, name=f"acc1_{e}{b}")
-                for t in range(PACK):
-                    nc.tensor.matmul_mx(
-                        out=acc[:, t, :],
-                        lhsT=wpw[:, e, 2 * P * t:2 * P * (t + 1)].bitcast(FP4X4),
-                        lhsT_scale=wps[:, e, P * t:P * (t + 1)],
-                        rhs=gw[1, e][:, cols].bitcast(FP8X4),
-                        rhs_scale=gs[1, e][:, cols],
-                        start=True,
-                        stop=False,
-                    )
-                    nc.tensor.matmul_mx(
-                        out=acc[:, t, :],
-                        lhsT=codes["a", e][:, P * t:P * (t + 1)].bitcast(FP8X4),
-                        lhsT_scale=scales["a", e][:, P * t:P * (t + 1)],
-                        rhs=gw[0, e][:, cols].bitcast(FP8X4),
-                        rhs_scale=gs[0, e][:, cols],
-                        start=False,
-                        stop=True,
-                    )
-                hb = shared.tile([P, BLK, PACK], BF16, name=f"hb{e}{b}", align_bytes=64, offset=1024 * (2 * e + b))
-                nc.scalar.activation(hb[:], acc[:].rearrange("p t s -> p s t"), GELU)
-                hc[e, b] = sb(f"hc{e}{b}", [P, BLK], U32)
-                hs[e, b] = sb(f"hs{e}{b}", [P, BLK], U8)
-                nc.vector.quantize_mx(
-                    out=hc[e, b][:].bitcast(FP8X4), scales=hs[e, b][:], in_=hb[:].rearrange("p s t -> p (s t)")
-                )
+        def quant_h(e, s0, s1):
+            nc.vector.quantize_mx(
+                out=hc[e][:, s0:s1].bitcast(FP8X4),
+                scales=hs[e][:, s0:s1],
+                in_=hb[e][:, s0:s1, :].rearrange("p s t -> p (s t)"),
+            )
 
         yc = sb("yc", [P, E * C], U32)
         ysc = sb("ysc", [P, E * C], U8)
+        y = [sb(f"y{e}", [P, PACK, C], F32) for e in range(E)]
+        yb = {(e, b): sb(f"yb{e}{b}", [P, BLK, PACK], BF16) for e in range(E) for b in range(2)}
         out_rows = out_0.rearrange("(p t) s -> p t s", t=PACK)
         out_words = out_1[0].rearrange("p s d -> p (s d)").bitcast(I32)
+        acc2 = {}
 
-        def layer2(e):
-            for b in range(C // BLK):
-                cols = slice(b * BLK, (b + 1) * BLK)
-                acc = psum.tile([P, PACK, BLK], F32, name=f"acc2_{e}{b}")
-                for t in range(PACK):
-                    nc.tensor.matmul_mx(
-                        out=acc[:, t, :],
-                        lhsT=codes["b", e][:, P * t:P * (t + 1)].bitcast(FP8X4),
-                        lhsT_scale=scales["b", e][:, P * t:P * (t + 1)],
-                        rhs=hc[e, b][:].bitcast(FP8X4),
-                        rhs_scale=hs[e, b][:],
-                        start=True,
-                        stop=True,
-                    )
-                g = slice(e * C + b * BLK, e * C + (b + 1) * BLK)
-                y = sb(f"y{e}{b}", [P, PACK, BLK], F32)
-                if (e, b) == (1, 0):
-                    nc.vector.tensor_copy(y[:], acc[:])
-                else:
-                    nc.scalar.copy(y[:], acc[:])
-                nc.sync.dma_start(out_rows[:, :, g], y[:])
-                yb = sb(f"yb{e}{b}", [P, BLK, PACK], BF16)
-                if e == 0:
-                    nc.scalar.copy(yb[:], acc[:].rearrange("p t s -> p s t"))
-                else:
-                    nc.vector.tensor_copy(
-                        yb[:].rearrange("p (c i) t -> p c t i", i=4),
-                        y[:].rearrange("p t (c i) -> p c t i", i=4),
-                    )
-                nc.vector.quantize_mx(
-                    out=yc[:, g].bitcast(FP8X4), scales=ysc[:, g], in_=yb[:].rearrange("p s t -> p (s t)")
+        def pass2(e, t, out, s0, s1):
+            nc.tensor.matmul_mx(
+                out=out,
+                lhsT=codes["b", e, t // 2][:, P * (t % 2):P * (t % 2 + 1)].bitcast(FP8X4),
+                lhsT_scale=scales["b", e, t // 2][:, P * (t % 2):P * (t % 2 + 1)],
+                rhs=hc[e][:, s0:s1].bitcast(FP8X4),
+                rhs_scale=hs[e][:, s0:s1],
+                start=True,
+                stop=True,
+            )
+
+        def layer2_rows(e, t0, t1, bank):
+            acc = psum.tile([P, t1 - t0, C], F32, name=bank)
+            for t in range(t0, t1):
+                pass2(e, t, acc[:, t - t0, :], 0, C)
+            return acc
+
+        def round_y(e, b, copy):
+            copy(
+                yb[e, b][:].rearrange("p (c i) t -> p c t i", i=8),
+                y[e][:, :, b * BLK:(b + 1) * BLK].rearrange("p t (c i) -> p c t i", i=8),
+            )
+
+        def quant_y(e, b):
+            cols = slice(e * C + b * BLK, e * C + (b + 1) * BLK)
+            nc.vector.quantize_mx(
+                out=yc[:, cols].bitcast(FP8X4), scales=ysc[:, cols], in_=yb[e, b][:].rearrange("p s t -> p (s t)")
+            )
+
+        def warm_pe(n):
+            idle = psum.tile([P, E * C], F32, name="acc2_00")
+            for i in range(n):
+                nc.tensor.matmul_mx(
+                    out=idle[:],
+                    lhsT=gw[1][:, 0:P].bitcast(FP8X4),
+                    lhsT_scale=gs0[:, 0:P],
+                    rhs=gw[0][:].bitcast(FP8X4),
+                    rhs_scale=gs0[:],
+                    start=True,
+                    stop=True,
                 )
-            ecols = slice(e * C, (e + 1) * C)
-            nc.sync.dma_start(out_words[:, ecols], yc[:, ecols].bitcast(I32))
+
+        def store_words(s0, s1):
+            nc.sync.dma_start(out_words[:, s0:s1], yc[:, s0:s1].bitcast(I32))
 
         s_copy = nc.scalar.copy
         v_copy = nc.vector.tensor_copy
-        M = HALF // PACK
 
-        for e in range(E):
-            gather_words(0, e)
-        for e in range(E):
-            gather_scales(0, e)
-        gather_words(1, 0)
-        gather_scales(1, 0)
+        gather_scales(gs0[:], 0, 0, E * C)
+        gather_words(0, 0, E * C)
+        gather_words(1, 0, E * C)
+        warm_pe(3)
+        gather_scales(gs[1, 0], 1, 0, C)
+        deal_scales()
         deal_words()
-        cast("a", 0, 0, 0, M, s_copy)
-        cast("a", 0, 1, 0, M, s_copy)
-        quant_w("a", 0, 1)
-        deal_scales(0)
-        deal_scales(1)
-        gather_words(1, 1)
-        gather_scales(1, 1)
-        cast("a", 1, 0, 0, M, s_copy)
-        cast("a", 1, 1, 0, M, s_copy)
-        quant_w("a", 1, 1)
-        cast("b", 0, 0, 0, M, s_copy)
-        cast("b", 0, 1, 0, M, v_copy)
-        quant_w("b", 0, 1)
-        layer1(0)
-        cast("b", 1, 0, 0, M, v_copy)
-        cast("b", 1, 1, 0, M // 2, v_copy)
-        cast("b", 1, 2, 0, M // 2, v_copy)
-        quant_w("b", 1, 2)
-        layer1(1)
-        layer2(0)
-        layer2(1)
+        cast_w1(0, 0, 4, s_copy)
+        quant_w("a", 0, 0, 2)
+        quant_w("a", 0, 2, 4)
+        cast_w1(1, 0, 2, s_copy)
+        cast_w1(1, 2, 4, v_copy)
+        quant_w("a", 1, 2, 4)
+        gather_scales(gs[1, 1], 1, C, E * C)
+        quant_w("a", 1, 0, 2)
+        for b in range(2):
+            layer1(0, b)
+            gelu(0, b)
+        cast_w2(0, 0, 2, s_copy)
+        for b in range(2):
+            layer1(1, b)
+            gelu(1, b)
+        quant_h(0, 0, BLK)
+        quant_h(0, BLK, C)
+        cast_w2(0, 2, 4, v_copy)
+        quant_w("b", 0, 2, 4)
+        quant_w("b", 0, 0, 2)
+        for c in range(2):
+            cast_last(c, 0, 2, v_copy)
+            cast_last(c, 2, 4, v_copy)
+        quant_w("b", 1, 0, 2)
+        quant_h(1, 0, C)
+        quant_w("b", 1, 2, 3)
+        quant_w("b", 1, 3, 4)
+        for u in (1, 0):
+            s_copy(y[0][:, 2 * u:2 * u + 2, :], layer2_rows(0, 2 * u, 2 * u + 2, f"acc2_0{u}")[:])
+            nc.sync.dma_start(out_rows[:, 2 * u:2 * u + 2, 0:C], y[0][:, 2 * u:2 * u + 2, :])
+        s_copy(y[1][:, 0:2, :], layer2_rows(1, 0, 2, "acc2_1")[:])
+        nc.sync.dma_start(out_rows[:, 0:2, C:2 * C], y[1][:, 0:2, :])
+        round_y(0, 0, v_copy)
+        s_copy(y[1][:, 2:3, :], layer2_rows(1, 2, 3, "acc2_2")[:])
+        v_copy(y[1][:, 3:4, :], layer2_rows(1, 3, 4, "acc1_00")[:])
+        nc.sync.dma_start(out_rows[:, 2:4, C:2 * C], y[1][:, 2:4, :])
+        round_y(0, 1, v_copy)
+        round_y(1, 0, v_copy)
+        round_y(1, 1, s_copy)
+        quant_y(0, 0)
+        quant_y(0, 1)
+        quant_y(1, 0)
+        store_words(0, C + BLK)
+        quant_y(1, 1)
+        store_words(C + BLK, 2 * C)
         for q in range(4):
             eng = nc.sync if q % 2 == 0 else nc.scalar
             eng.dma_start(out_2[0, 4 * q:4 * q + 4, :].bitcast(I32), ysc[32 * q:32 * q + 4, :].bitcast(I32))

@@ -31,11 +31,10 @@ def tile_moe_duo_s_gelu_kernel(
         psum = ctx.enter_context(tc.psum_pool(name="psum", bufs=1))
 
         offsets = {
-            "raw_b0": 0, "hb1": 0,
-            "raw_b11": 12288, "hc1": 12288, "hs1": 13312, "yb00": 14336, "yb01": 15360,
-            "codes_b11": 8192, "ysc": 8192,
-            "raw_a1": 24576, "hb0": 24576, "gs11": 28672,
-            "wpw_raw": 34816, "scales_a00": 34816, "scales_a01": 35840,
+            "raw_b0": 0, "hc1": 0, "hs1": 1024, "hc0": 2048, "hs0": 3072,
+            "raw_b10": 8192, "y0": 8192,
+            "raw_b11": 12288, "ysc": 12288, "yb0": 13312,
+            "raw_a1": 24576, "hb0": 24576,
         }
 
         def sb(name, shape, dtype):
@@ -89,9 +88,8 @@ def tile_moe_duo_s_gelu_kernel(
 
         gw = [sb(f"gw{li}", [P, E * C], U32) for li in range(2)]
         gs0 = sb("gs0", [P, E * C], U8)
-        gs = {(0, e): gs0[:, e * C:(e + 1) * C] for e in range(E)}
-        for e in range(E):
-            gs[1, e] = sb(f"gs1{e}", [P, C], U8)[:]
+        gs1 = sb("gs1", [P, E * C], U8)
+        gs = {(li, e): (gs0, gs1)[li][:, e * C:(e + 1) * C] for li in range(2) for e in range(E)}
 
         def gather_words(li, s0, s1):
             nc.vector.tensor_copy(gw[li][:, s0:s1], xw[:].indirect(lists[li][:, s0 // 16:s1 // 16]))
@@ -103,15 +101,15 @@ def tile_moe_duo_s_gelu_kernel(
         wps = sb("wps", [P, E, H], U8)
 
         def deal_words():
-            nc.vector.tensor_copy(
+            nc.gpsimd.tensor_copy(
                 wpw[:].bitcast(I32).rearrange("p e (t b i) -> p e b t i", t=PACK, i=4),
                 wpw_raw[:].bitcast(I32).rearrange("p e (b i t) -> p e b t i", t=PACK, i=4),
             )
 
         def deal_scales():
-            nc.vector.tensor_copy(
-                wps[:].bitcast(U16).rearrange("p e (t b i) -> p e b t i", t=PACK, i=8),
-                wps_raw[:].bitcast(U16).rearrange("p e (b i t) -> p e b t i", t=PACK, i=8),
+            nc.gpsimd.tensor_copy(
+                wps[:].rearrange("p e (t q r) -> p e t q r", t=PACK, r=2),
+                wps_raw[:].rearrange("p e (q t r) -> p e t q r", t=PACK, r=2),
             )
 
         grouped = {}
@@ -156,11 +154,12 @@ def tile_moe_duo_s_gelu_kernel(
         hs = [sb(f"hs{e}", [P, C], U8) for e in range(E)]
         acc1 = {}
 
-        def layer1(e, b):
+        def layer1(e, b, u):
             cols = slice(e * C + b * BLK, e * C + (b + 1) * BLK)
-            acc = psum.tile([P, PACK, BLK], F32, name=f"acc1_{e}{b}")
-            acc1[e, b] = acc
-            for t in range(PACK):
+            if (e, b) not in acc1:
+                acc1[e, b] = psum.tile([P, PACK, BLK], F32, name=f"acc1_{e}{b}")
+            acc = acc1[e, b]
+            for t in (2 * u, 2 * u + 1):
                 nc.tensor.matmul_mx(
                     out=acc[:, t, :],
                     lhsT=wpw[:, e, 2 * P * t:2 * P * (t + 1)].bitcast(FP4X4),
@@ -193,7 +192,9 @@ def tile_moe_duo_s_gelu_kernel(
         yc = sb("yc", [P, E * C], U32)
         ysc = sb("ysc", [P, E * C], U8)
         y = [sb(f"y{e}", [P, PACK, C], F32) for e in range(E)]
-        yb = {(e, b): sb(f"yb{e}{b}", [P, BLK, PACK], BF16) for e in range(E) for b in range(2)}
+        yb = {(0, 0, C): sb("yb0", [P, C, PACK], BF16)}
+        for b in range(2):
+            yb[1, b * BLK, (b + 1) * BLK] = sb(f"yb1{b}", [P, BLK, PACK], BF16)
         out_rows = out_0.rearrange("(p t) s -> p t s", t=PACK)
         out_words = out_1[0].rearrange("p s d -> p (s d)").bitcast(I32)
         acc2 = {}
@@ -215,25 +216,25 @@ def tile_moe_duo_s_gelu_kernel(
                 pass2(e, t, acc[:, t - t0, :], 0, C)
             return acc
 
-        def round_y(e, b, copy):
+        def round_y(e, s0, s1, copy):
             copy(
-                yb[e, b][:].rearrange("p (c i) t -> p c t i", i=8),
-                y[e][:, :, b * BLK:(b + 1) * BLK].rearrange("p t (c i) -> p c t i", i=8),
+                yb[e, s0, s1][:].rearrange("p (c i) t -> p c t i", i=8),
+                y[e][:, :, s0:s1].rearrange("p t (c i) -> p c t i", i=8),
             )
 
-        def quant_y(e, b):
-            cols = slice(e * C + b * BLK, e * C + (b + 1) * BLK)
+        def quant_y(e, s0, s1):
+            cols = slice(e * C + s0, e * C + s1)
             nc.vector.quantize_mx(
-                out=yc[:, cols].bitcast(FP8X4), scales=ysc[:, cols], in_=yb[e, b][:].rearrange("p s t -> p (s t)")
+                out=yc[:, cols].bitcast(FP8X4), scales=ysc[:, cols], in_=yb[e, s0, s1][:].rearrange("p s t -> p (s t)")
             )
 
-        def warm_pe(n):
-            idle = psum.tile([P, E * C], F32, name="acc2_00")
+        def warm_pe(n, words, plane):
+            idle = psum.tile([P, E * C], F32, name="acc2_2")
             for i in range(n):
                 nc.tensor.matmul_mx(
                     out=idle[:],
-                    lhsT=gw[1][:, 0:P].bitcast(FP8X4),
-                    lhsT_scale=gs0[:, 0:P],
+                    lhsT=words[:, 0:P].bitcast(FP8X4),
+                    lhsT_scale=plane[:, 0:P],
                     rhs=gw[0][:].bitcast(FP8X4),
                     rhs_scale=gs0[:],
                     start=True,
@@ -246,57 +247,54 @@ def tile_moe_duo_s_gelu_kernel(
         s_copy = nc.scalar.copy
         v_copy = nc.vector.tensor_copy
 
-        gather_scales(gs0[:], 0, 0, E * C)
         gather_words(0, 0, E * C)
+        gather_scales(gs0[:], 0, 0, E * C)
         gather_words(1, 0, E * C)
-        warm_pe(3)
-        gather_scales(gs[1, 0], 1, 0, C)
+        warm_pe(2, gw[1], gs0)
+        gather_scales(gs1[:], 1, 0, E * C)
         deal_scales()
         deal_words()
-        cast_w1(0, 0, 4, s_copy)
+        cast_w1(0, 0, 2, s_copy)
+        cast_w1(0, 2, 4, s_copy)
         quant_w("a", 0, 0, 2)
         quant_w("a", 0, 2, 4)
         cast_w1(1, 0, 2, s_copy)
         cast_w1(1, 2, 4, v_copy)
         quant_w("a", 1, 2, 4)
-        gather_scales(gs[1, 1], 1, C, E * C)
         quant_w("a", 1, 0, 2)
-        for b in range(2):
-            layer1(0, b)
-            gelu(0, b)
-        cast_w2(0, 0, 2, s_copy)
-        for b in range(2):
-            layer1(1, b)
-            gelu(1, b)
-        quant_h(0, 0, BLK)
-        quant_h(0, BLK, C)
+        for e in range(E):
+            for b in range(2):
+                layer1(e, b, e)
+            for b in range(2):
+                layer1(e, b, 1 - e)
+                gelu(e, b)
+        cast_w2(0, 0, 2, v_copy)
         cast_w2(0, 2, 4, v_copy)
-        quant_w("b", 0, 2, 4)
         quant_w("b", 0, 0, 2)
-        for c in range(2):
-            cast_last(c, 0, 2, v_copy)
-            cast_last(c, 2, 4, v_copy)
-        quant_w("b", 1, 0, 2)
+        warm_pe(1, codes["b", 0, 0], scales["b", 0, 0])
+        quant_h(0, 0, C)
+        quant_w("b", 0, 2, 4)
         quant_h(1, 0, C)
-        quant_w("b", 1, 2, 3)
-        quant_w("b", 1, 3, 4)
-        for u in (1, 0):
+        for c in range(2):
+            cast_last(c, 0, 2, (s_copy, v_copy)[c])
+            cast_last(c, 2, 4, (s_copy, v_copy)[c])
+        quant_w("b", 1, 0, 2)
+        quant_w("b", 1, 2, 4)
+        for u in (0, 1):
             s_copy(y[0][:, 2 * u:2 * u + 2, :], layer2_rows(0, 2 * u, 2 * u + 2, f"acc2_0{u}")[:])
             nc.sync.dma_start(out_rows[:, 2 * u:2 * u + 2, 0:C], y[0][:, 2 * u:2 * u + 2, :])
+        round_y(0, 0, C, v_copy)
         s_copy(y[1][:, 0:2, :], layer2_rows(1, 0, 2, "acc2_1")[:])
         nc.sync.dma_start(out_rows[:, 0:2, C:2 * C], y[1][:, 0:2, :])
-        round_y(0, 0, v_copy)
-        s_copy(y[1][:, 2:3, :], layer2_rows(1, 2, 3, "acc2_2")[:])
-        v_copy(y[1][:, 3:4, :], layer2_rows(1, 3, 4, "acc1_00")[:])
+        v_copy(y[1][:, 2:3, :], layer2_rows(1, 2, 3, "acc2_2")[:])
+        s_copy(y[1][:, 3:4, :], layer2_rows(1, 3, 4, "acc1_00")[:])
         nc.sync.dma_start(out_rows[:, 2:4, C:2 * C], y[1][:, 2:4, :])
-        round_y(0, 1, v_copy)
-        round_y(1, 0, v_copy)
-        round_y(1, 1, s_copy)
-        quant_y(0, 0)
-        quant_y(0, 1)
-        quant_y(1, 0)
+        quant_y(0, 0, C)
+        round_y(1, 0, BLK, v_copy)
+        round_y(1, BLK, C, s_copy)
+        quant_y(1, 0, BLK)
         store_words(0, C + BLK)
-        quant_y(1, 1)
+        quant_y(1, BLK, C)
         store_words(C + BLK, 2 * C)
         for q in range(4):
             eng = nc.sync if q % 2 == 0 else nc.scalar

@@ -228,13 +228,13 @@ def tile_moe_duo_s_gelu_kernel(
                 out=yc[:, cols].bitcast(FP8X4), scales=ysc[:, cols], in_=yb[e, s0, s1][:].rearrange("p s t -> p (s t)")
             )
 
-        def warm_pe(n, words, plane):
+        def warm_pe(n, words, plane, m):
             idle = psum.tile([P, E * C], F32, name="acc2_2")
             for i in range(n):
                 nc.tensor.matmul_mx(
-                    out=idle[:],
-                    lhsT=words[:, 0:P].bitcast(FP8X4),
-                    lhsT_scale=plane[:, 0:P],
+                    out=idle[0:m, :],
+                    lhsT=words[:, 0:m].bitcast(FP8X4),
+                    lhsT_scale=plane[:, 0:m],
                     rhs=gw[0][:].bitcast(FP8X4),
                     rhs_scale=gs0[:],
                     start=True,
@@ -249,8 +249,8 @@ def tile_moe_duo_s_gelu_kernel(
 
         gather_words(0, 0, E * C)
         gather_scales(gs0[:], 0, 0, E * C)
+        warm_pe(3, gw[0], gs0, P // 2)
         gather_words(1, 0, E * C)
-        warm_pe(2, gw[1], gs0)
         gather_scales(gs1[:], 1, 0, E * C)
         deal_scales()
         deal_words()
@@ -271,7 +271,7 @@ def tile_moe_duo_s_gelu_kernel(
         cast_w2(0, 0, 2, v_copy)
         cast_w2(0, 2, 4, v_copy)
         quant_w("b", 0, 0, 2)
-        warm_pe(1, codes["b", 0, 0], scales["b", 0, 0])
+        warm_pe(1, codes["b", 0, 0], scales["b", 0, 0], P)
         quant_h(0, 0, C)
         quant_w("b", 0, 2, 4)
         quant_h(1, 0, C)

@@ -218,8 +218,8 @@ def tile_moe_duo_s_gelu_kernel(
 
         def round_y(e, s0, s1, copy):
             copy(
-                yb[e, s0, s1][:].rearrange("p (c i) t -> p c t i", i=8),
-                y[e][:, :, s0:s1].rearrange("p t (c i) -> p c t i", i=8),
+                yb[e, s0, s1][:].rearrange("p (c i) t -> p c t i", i=4),
+                y[e][:, :, s0:s1].rearrange("p t (c i) -> p c t i", i=4),
             )
 
         def quant_y(e, s0, s1):
@@ -249,7 +249,7 @@ def tile_moe_duo_s_gelu_kernel(
 
         gather_words(0, 0, E * C)
         gather_scales(gs0[:], 0, 0, E * C)
-        warm_pe(3, gw[0], gs0, P // 2)
+        warm_pe(4, gw[0], gs0, P // 2)
         gather_words(1, 0, E * C)
         gather_scales(gs1[:], 1, 0, E * C)
         deal_scales()
@@ -271,7 +271,6 @@ def tile_moe_duo_s_gelu_kernel(
         cast_w2(0, 0, 2, v_copy)
         cast_w2(0, 2, 4, v_copy)
         quant_w("b", 0, 0, 2)
-        warm_pe(1, codes["b", 0, 0], scales["b", 0, 0], P)
         quant_h(0, 0, C)
         quant_w("b", 0, 2, 4)
         quant_h(1, 0, C)

@@ -98,7 +98,7 @@ def tile_moe_duo_s_gelu_kernel(
             nc.vector.tensor_copy(out, xs[:].indirect(lists[li][:, s0 // 16:s1 // 16]))
 
         wpw = sb("wpw", [P, E, 2 * H], U8)
-        wps = sb("wps", [P, E, H], U8)
+        wps = [sb(f"wps{e}", [P, H], U8) for e in range(E)]
 
         def deal_words():
             nc.gpsimd.tensor_copy(
@@ -106,10 +106,16 @@ def tile_moe_duo_s_gelu_kernel(
                 wpw_raw[:].bitcast(I32).rearrange("p e (b i t) -> p e b t i", t=PACK, i=4),
             )
 
-        def deal_scales():
+        def deal_scale_bytes(e):
             nc.gpsimd.tensor_copy(
-                wps[:].rearrange("p e (t q r) -> p e t q r", t=PACK, r=2),
-                wps_raw[:].rearrange("p e (q t r) -> p e t q r", t=PACK, r=2),
+                wps[e][:].rearrange("p (t q r) -> p t q r", t=PACK, r=2),
+                wps_raw[:, e].rearrange("p (q t r) -> p t q r", t=PACK, r=2),
+            )
+
+        def deal_scale_pairs(e):
+            nc.vector.tensor_copy(
+                wps[e][:].bitcast(U16).rearrange("p (t b i) -> p b t i", t=PACK, i=8),
+                wps_raw[:, e].bitcast(U16).rearrange("p (b i t) -> p b t i", t=PACK, i=8),
             )
 
         grouped = {}
@@ -163,7 +169,7 @@ def tile_moe_duo_s_gelu_kernel(
                 nc.tensor.matmul_mx(
                     out=acc[:, t, :],
                     lhsT=wpw[:, e, 2 * P * t:2 * P * (t + 1)].bitcast(FP4X4),
-                    lhsT_scale=wps[:, e, P * t:P * (t + 1)],
+                    lhsT_scale=wps[e][:, P * t:P * (t + 1)],
                     rhs=gw[1][:, cols].bitcast(FP8X4),
                     rhs_scale=gs[1, e][:, b * BLK:(b + 1) * BLK],
                     start=True,
@@ -252,12 +258,13 @@ def tile_moe_duo_s_gelu_kernel(
         warm_pe(4, gw[0], gs0, P // 2)
         gather_words(1, 0, E * C)
         gather_scales(gs1[:], 1, 0, E * C)
-        deal_scales()
+        deal_scale_bytes(0)
         deal_words()
         cast_w1(0, 0, 2, s_copy)
         cast_w1(0, 2, 4, s_copy)
         quant_w("a", 0, 0, 2)
         quant_w("a", 0, 2, 4)
+        deal_scale_pairs(1)
         cast_w1(1, 0, 2, s_copy)
         cast_w1(1, 2, 4, v_copy)
         quant_w("a", 1, 2, 4)
@@ -274,9 +281,9 @@ def tile_moe_duo_s_gelu_kernel(
         quant_h(0, 0, C)
         quant_w("b", 0, 2, 4)
         quant_h(1, 0, C)
-        for c in range(2):
-            cast_last(c, 0, 2, (s_copy, v_copy)[c])
-            cast_last(c, 2, 4, (s_copy, v_copy)[c])
+        cast_last(0, 0, 4, s_copy)
+        cast_last(1, 0, 2, v_copy)
+        cast_last(1, 2, 4, v_copy)
         quant_w("b", 1, 0, 2)
         quant_w("b", 1, 2, 4)
         for u in (0, 1):

@@ -19,6 +19,7 @@ P = 128
 PACK = 4
 BLK = 128
 WIN = 704
+CUT = 192
 
 
 def tile_moe_duo_s_gelu_kernel(
@@ -31,7 +32,7 @@ def tile_moe_duo_s_gelu_kernel(
         psum = ctx.enter_context(tc.psum_pool(name="psum", bufs=1))
 
         offsets = {
-            "raw_b0": 0, "hc1": 0, "hs1": 1024, "hc0": 2048, "hs0": 3072,
+            "raw_b0": 0, "hc1": 0, "hs1": 1024, "hc01": 2048, "hs01": 3072,
             "raw_b10": 8192, "y0": 8192,
             "raw_b11": 12288, "ysc": 12288, "yb0": 13312,
             "raw_a1": 24576, "hb0": 24576,
@@ -57,7 +58,8 @@ def tile_moe_duo_s_gelu_kernel(
         raw = {}
         for which, e in (("a", 0), ("a", 1), ("b", 0)):
             raw[which, e] = sb(f"raw_{which}{e}", [P, PACK, H], F32)
-        last = [sb(f"raw_b1{c}", [P, PACK, N // 2], F32) for c in range(2)]
+        cuts = (0, CUT, N)
+        last = [sb(f"raw_b1{c}", [P, PACK, cuts[c + 1] - cuts[c]], F32) for c in range(2)]
 
         def load_w1(e):
             nc.sync.dma_start(raw["a", e][:], w1[e].rearrange("(p j) c -> p j c", j=PACK))
@@ -83,7 +85,7 @@ def tile_moe_duo_s_gelu_kernel(
         load_w1(1)
         load_w2(0, raw["b", 0], 0, N)
         for c in range(2):
-            load_w2(1, last[c], c * N // 2, (c + 1) * N // 2)
+            load_w2(1, last[c], cuts[c], cuts[c + 1])
         nc.scalar.activation(warm_out[:], warm[:], GELU)
 
         gw = [sb(f"gw{li}", [P, E * C], U32) for li in range(2)]
@@ -144,7 +146,7 @@ def tile_moe_duo_s_gelu_kernel(
 
         def cast_last(c, t0, t1, copy):
             copy(
-                grouped["b", 1][:, t0:t1, c * P // 2:(c + 1) * P // 2].rearrange("p t m j -> p m j t"),
+                grouped["b", 1][:, t0:t1, cuts[c] // PACK:cuts[c + 1] // PACK].rearrange("p t m j -> p m j t"),
                 last[c][:].rearrange("p j (m t) -> p m j t", t=PACK)[:, :, :, t0:t1],
             )
 
@@ -156,8 +158,11 @@ def tile_moe_duo_s_gelu_kernel(
             )
 
         hb = [sb(f"hb{e}", [P, C, PACK], BF16) for e in range(E)]
-        hc = [sb(f"hc{e}", [P, C], U32) for e in range(E)]
-        hs = [sb(f"hs{e}", [P, C], U8) for e in range(E)]
+        hc = {(1, 0, C): sb("hc1", [P, C], U32)}
+        hs = {(1, 0, C): sb("hs1", [P, C], U8)}
+        for b in range(2):
+            hc[0, b * BLK, (b + 1) * BLK] = sb(f"hc0{b}", [P, BLK], U32)
+            hs[0, b * BLK, (b + 1) * BLK] = sb(f"hs0{b}", [P, BLK], U8)
         acc1 = {}
 
         def layer1(e, b, u):
@@ -190,8 +195,8 @@ def tile_moe_duo_s_gelu_kernel(
 
         def quant_h(e, s0, s1):
             nc.vector.quantize_mx(
-                out=hc[e][:, s0:s1].bitcast(FP8X4),
-                scales=hs[e][:, s0:s1],
+                out=hc[e, s0, s1][:].bitcast(FP8X4),
+                scales=hs[e, s0, s1][:],
                 in_=hb[e][:, s0:s1, :].rearrange("p s t -> p (s t)"),
             )
 
@@ -210,8 +215,8 @@ def tile_moe_duo_s_gelu_kernel(
                 out=out,
                 lhsT=codes["b", e, t // 2][:, P * (t % 2):P * (t % 2 + 1)].bitcast(FP8X4),
                 lhsT_scale=scales["b", e, t // 2][:, P * (t % 2):P * (t % 2 + 1)],
-                rhs=hc[e][:, s0:s1].bitcast(FP8X4),
-                rhs_scale=hs[e][:, s0:s1],
+                rhs=hc[e, s0, s1][:].bitcast(FP8X4),
+                rhs_scale=hs[e, s0, s1][:],
                 start=True,
                 stop=True,
             )
@@ -219,7 +224,9 @@ def tile_moe_duo_s_gelu_kernel(
         def layer2_rows(e, t0, t1, bank):
             acc = psum.tile([P, t1 - t0, C], F32, name=bank)
             for t in range(t0, t1):
-                pass2(e, t, acc[:, t - t0, :], 0, C)
+                for he, s0, s1 in hc:
+                    if he == e:
+                        pass2(e, t, acc[:, t - t0, s0:s1], s0, s1)
             return acc
 
         def round_y(e, s0, s1, copy):
@@ -255,7 +262,7 @@ def tile_moe_duo_s_gelu_kernel(
 
         gather_words(0, 0, E * C)
         gather_scales(gs0[:], 0, 0, E * C)
-        warm_pe(4, gw[0], gs0, P // 2)
+        warm_pe(3, gw[0], gs0, P // 2)
         gather_words(1, 0, E * C)
         gather_scales(gs1[:], 1, 0, E * C)
         deal_scale_bytes(0)
@@ -275,13 +282,16 @@ def tile_moe_duo_s_gelu_kernel(
             for b in range(2):
                 layer1(e, b, 1 - e)
                 gelu(e, b)
+        quant_h(0, 0, BLK)
         cast_w2(0, 0, 2, v_copy)
         cast_w2(0, 2, 4, v_copy)
         quant_w("b", 0, 0, 2)
-        quant_h(0, 0, C)
+        warm_pe(1, codes["b", 0, 0], scales["b", 0, 0], P)
+        quant_h(0, BLK, C)
         quant_w("b", 0, 2, 4)
         quant_h(1, 0, C)
-        cast_last(0, 0, 4, s_copy)
+        cast_last(0, 0, 2, s_copy)
+        cast_last(0, 2, 4, s_copy)
         cast_last(1, 0, 2, v_copy)
         cast_last(1, 2, 4, v_copy)
         quant_w("b", 1, 0, 2)

@@ -230,8 +230,9 @@ def tile_moe_duo_s_gelu_kernel(
             return acc
 
         def round_y(e, s0, s1, copy):
+            lo, hi = [(a, b) for ye, a, b in yb if ye == e and a <= s0 < b][0]
             copy(
-                yb[e, s0, s1][:].rearrange("p (c i) t -> p c t i", i=4),
+                yb[e, lo, hi][:, s0 - lo:s1 - lo].rearrange("p (c i) t -> p c t i", i=4),
                 y[e][:, :, s0:s1].rearrange("p t (c i) -> p c t i", i=4),
             )
 
@@ -273,8 +274,10 @@ def tile_moe_duo_s_gelu_kernel(
         quant_w("a", 0, 2, 4)
         deal_scale_pairs(1)
         cast_w1(1, 0, 2, s_copy)
-        cast_w1(1, 2, 4, v_copy)
-        quant_w("a", 1, 2, 4)
+        cast_w1(1, 2, 3, v_copy)
+        cast_w1(1, 3, 4, v_copy)
+        quant_w("a", 1, 2, 3)
+        quant_w("a", 1, 3, 4)
         quant_w("a", 1, 0, 2)
         for e in range(E):
             for b in range(2):
@@ -294,20 +297,23 @@ def tile_moe_duo_s_gelu_kernel(
         cast_last(0, 2, 4, s_copy)
         cast_last(1, 0, 2, v_copy)
         cast_last(1, 2, 4, v_copy)
-        quant_w("b", 1, 0, 2)
+        quant_w("b", 1, 0, 1)
+        quant_w("b", 1, 1, 2)
         quant_w("b", 1, 2, 4)
         for u in (0, 1):
             s_copy(y[0][:, 2 * u:2 * u + 2, :], layer2_rows(0, 2 * u, 2 * u + 2, f"acc2_0{u}")[:])
             nc.sync.dma_start(out_rows[:, 2 * u:2 * u + 2, 0:C], y[0][:, 2 * u:2 * u + 2, :])
         round_y(0, 0, C, v_copy)
-        s_copy(y[1][:, 0:2, :], layer2_rows(1, 0, 2, "acc2_1")[:])
+        s_copy(y[1][:, 0:1, :], layer2_rows(1, 0, 1, "acc2_1")[:])
+        s_copy(y[1][:, 1:2, :], layer2_rows(1, 1, 2, "acc1_01")[:])
         nc.sync.dma_start(out_rows[:, 0:2, C:2 * C], y[1][:, 0:2, :])
         v_copy(y[1][:, 2:3, :], layer2_rows(1, 2, 3, "acc2_2")[:])
         s_copy(y[1][:, 3:4, :], layer2_rows(1, 3, 4, "acc1_00")[:])
         nc.sync.dma_start(out_rows[:, 2:4, C:2 * C], y[1][:, 2:4, :])
         quant_y(0, 0, C)
         round_y(1, 0, BLK, v_copy)
-        round_y(1, BLK, C, s_copy)
+        round_y(1, BLK, BLK + BLK // 2, v_copy)
+        round_y(1, BLK + BLK // 2, C, s_copy)
         quant_y(1, 0, BLK)
         store_words(0, C + BLK)
         quant_y(1, BLK, C)

@@ -263,7 +263,7 @@ def tile_moe_duo_s_gelu_kernel(
 
         gather_words(0, 0, E * C)
         gather_scales(gs0[:], 0, 0, E * C)
-        warm_pe(3, gw[0], gs0, P // 2)
+        warm_pe(3, gw[0], gs0, P // 4)
         gather_words(1, 0, E * C)
         gather_scales(gs1[:], 1, 0, E * C)
         deal_scale_bytes(0)
@@ -289,7 +289,7 @@ def tile_moe_duo_s_gelu_kernel(
         cast_w2(0, 0, 2, v_copy)
         cast_w2(0, 2, 4, v_copy)
         quant_w("b", 0, 0, 2)
-        warm_pe(1, codes["b", 0, 0], scales["b", 0, 0], P)
+        warm_pe(1, codes["b", 0, 0], scales["b", 0, 0], P // 4)
         quant_h(0, BLK, C)
         quant_w("b", 0, 2, 4)
         quant_h(1, 0, C)

@@ -319,5 +319,4 @@ def tile_moe_duo_s_gelu_kernel(
         quant_y(1, BLK, C)
         store_words(C + BLK, 2 * C)
         for q in range(4):
-            eng = nc.sync if q % 2 == 0 else nc.scalar
-            eng.dma_start(out_2[0, 4 * q:4 * q + 4, :].bitcast(I32), ysc[32 * q:32 * q + 4, :].bitcast(I32))
+            nc.sync.dma_start(out_2[0, 4 * q:4 * q + 4, :].bitcast(I32), ysc[32 * q:32 * q + 4, :].bitcast(I32))

@@ -40,8 +40,8 @@ def tile_moe_duo_s_gelu_kernel(
 
         def sb(name, shape, dtype):
             if name in offsets:
-                return shared.tile(shape, dtype, name=name, align_bytes=64, offset=offsets[name])
-            return keep.tile(shape, dtype, name=name, align_bytes=64)
+                return shared.tile(shape, dtype, name=name, align_bytes=256, offset=offsets[name])
+            return keep.tile(shape, dtype, name=name, align_bytes=256)
 
         lists = [keep.tile([P, E * C // 16], U16, name="offs_sb"), keep.tile([P, E * C // 16], U16, name="offs2_sb")]
         xw = sb("xw", [P, WIN], U32)

from contextlib import ExitStack

import concourse.mybir as mybir

K, T, E, C, H, N = 512, 512, 2, 256, 512, 512
FLOPS = 2 * E * C * (2 * K * H + H * N)

F32 = mybir.dt.float32
BF16 = mybir.dt.bfloat16
I32 = mybir.dt.int32
U32 = mybir.dt.uint32
U16 = mybir.dt.uint16
U8 = mybir.dt.uint8
FP8X4 = mybir.dt.float8_e4m3fn_x4
FP4X4 = mybir.dt.float4_e2m1fn_x4
GELU = mybir.ActivationFunctionType.Gelu_apprx_tanh

P = 128
PACK = 4
BLK = 128
WIN = 704
CUT = 192


def tile_moe_duo_s_gelu_kernel(
    tc, x_words, x_scales, w1, wp_words, wp_scales, w2, offs, offs2, out_0, out_1, out_2
):
    nc = tc.nc
    with ExitStack() as ctx:
        keep = ctx.enter_context(tc.tile_pool(name="keep", bufs=1))
        shared = ctx.enter_context(tc.tile_pool(name="shared", bufs=1))
        psum = ctx.enter_context(tc.psum_pool(name="psum", bufs=1))

        offsets = {
            "raw_b0": 0, "hc1": 0, "hs1": 1024, "hc01": 2048, "hs01": 3072,
            "raw_b10": 8192, "y0": 8192,
            "raw_b11": 12288, "ysc": 12288, "yb0": 13312,
            "raw_a1": 24576, "hb0": 24576,
        }

        def sb(name, shape, dtype):
            if name in offsets:
                return shared.tile(shape, dtype, name=name, align_bytes=256, offset=offsets[name])
            return keep.tile(shape, dtype, name=name, align_bytes=256)

        lists = [keep.tile([P, E * C // 16], U16, name="offs_sb"), keep.tile([P, E * C // 16], U16, name="offs2_sb")]
        xw = sb("xw", [P, WIN], U32)
        xs = sb("xs", [P, WIN], U8)
        wps_raw = sb("wps_raw", [P, E, H], U8)
        wpw_raw = sb("wpw_raw", [P, E, 2 * H], U8)
        warm = sb("warm", [P, 8], F32)
        warm_out = sb("warm_out", [P, 8], F32)
        nc.gpsimd.memset(xs[:].bitcast(I32), 0)
        nc.gpsimd.memset(warm[:], 0.0)
        nc.vector.memset(xw[:, T:].bitcast(I32), 0)
        nc.vector.memset(wps_raw[:].bitcast(I32), 0)

        raw = {}
        for which, e in (("a", 0), ("a", 1), ("b", 0)):
            raw[which, e] = sb(f"raw_{which}{e}", [P, PACK, H], F32)
        cuts = (0, CUT, N)
        last = [sb(f"raw_b1{c}", [P, PACK, cuts[c + 1] - cuts[c]], F32) for c in range(2)]

        def load_w1(e):
            nc.sync.dma_start(raw["a", e][:], w1[e].rearrange("(p j) c -> p j c", j=PACK))

        def load_w2(e, tile, c0, c1):
            rows = w2[e].rearrange("(q j r) c -> r q j c", j=PACK, r=2)
            for r in range(2):
                nc.sync.dma_start(tile[r:P:2], rows[r][:, :, c0:c1])

        nc.sync.dma_start(xw[:, :T].bitcast(I32), x_words[0].rearrange("p t d -> p (t d)").bitcast(I32))
        nc.sync.dma_start(lists[0][:], offs)
        for q in range(4):
            eng = nc.scalar if q < 2 else nc.sync
            eng.dma_start(xs[32 * q:32 * q + 4, :T].bitcast(I32), x_scales[0, 4 * q:4 * q + 4, :].bitcast(I32))
        nc.sync.dma_start(lists[1][:], offs2)
        load_w1(0)
        for q in range(4):
            nc.sync.dma_start(
                wps_raw[32 * q:32 * q + 4, :, :].bitcast(I32),
                wp_scales[:, 0, 4 * q:4 * q + 4, :].rearrange("e r c -> r e c").bitcast(I32),
            )
        nc.sync.dma_start(wpw_raw[:].bitcast(I32), wp_words[:, 0].rearrange("e p c -> p e c").bitcast(I32))
        load_w1(1)
        load_w2(0, raw["b", 0], 0, N)
        for c in range(2):
            load_w2(1, last[c], cuts[c], cuts[c + 1])
        nc.scalar.activation(warm_out[:], warm[:], GELU)

        gw = [sb(f"gw{li}", [P, E * C], U32) for li in range(2)]
        gs0 = sb("gs0", [P, E * C], U8)
        gs1 = sb("gs1", [P, E * C], U8)
        gs = {(li, e): (gs0, gs1)[li][:, e * C:(e + 1) * C] for li in range(2) for e in range(E)}

        def gather_words(li, s0, s1):
            nc.vector.tensor_copy(gw[li][:, s0:s1], xw[:].indirect(lists[li][:, s0 // 16:s1 // 16]))

        def gather_scales(out, li, s0, s1):
            nc.vector.tensor_copy(out, xs[:].indirect(lists[li][:, s0 // 16:s1 // 16]))

        wpw = sb("wpw", [P, E, 2 * H], U8)
        wps = [sb(f"wps{e}", [P, H], U8) for e in range(E)]

        def deal_words():
            nc.gpsimd.tensor_copy(
                wpw[:].bitcast(I32).rearrange("p e (t b i) -> p e b t i", t=PACK, i=4),
                wpw_raw[:].bitcast(I32).rearrange("p e (b i t) -> p e b t i", t=PACK, i=4),
            )

        def deal_scale_bytes(e):
            nc.gpsimd.tensor_copy(
                wps[e][:].rearrange("p (t q r) -> p t q r", t=PACK, r=2),
                wps_raw[:, e].rearrange("p (q t r) -> p t q r", t=PACK, r=2),
            )

        def deal_scale_pairs(e):
            nc.vector.tensor_copy(
                wps[e][:].bitcast(U16).rearrange("p (t b i) -> p b t i", t=PACK, i=8),
                wps_raw[:, e].bitcast(U16).rearrange("p (b i t) -> p b t i", t=PACK, i=8),
            )

        grouped = {}
        codes = {}
        scales = {}
        for which in "ab":
            for e in range(E):
                grouped[which, e] = sb(f"grp_{which}{e}", [P, PACK, P, PACK], BF16)
                for u in range(2):
                    pair_codes = sb(f"codes_{which}{e}{u}", [P, 2 * P], U32)
                    pair_scales = sb(f"scales_{which}{e}{u}", [P, 2 * P], U8)
                    codes[which, e, u] = pair_codes
                    scales[which, e, u] = pair_scales

        def cast_w1(e, t0, t1, copy):
            copy(
                grouped["a", e][:, t0:t1].rearrange("p t (q r) j -> p q j t r", r=2),
                raw["a", e][:].rearrange("p j (q t r) -> p q j t r", t=PACK, r=2)[:, :, :, t0:t1, :],
            )

        def cast_w2(e, t0, t1, copy):
            copy(
                grouped["b", e][:, t0:t1].rearrange("p t m j -> p m j t"),
                raw["b", e][:].rearrange("p j (m t) -> p m j t", t=PACK)[:, :, :, t0:t1],
            )

        def cast_last(c, t0, t1, copy):
            copy(
                grouped["b", 1][:, t0:t1, cuts[c] // PACK:cuts[c + 1] // PACK].rearrange("p t m j -> p m j t"),
                last[c][:].rearrange("p j (m t) -> p m j t", t=PACK)[:, :, :, t0:t1],
            )

        def quant_w(which, e, t0, t1):
            nc.vector.quantize_mx(
                out=codes[which, e, t0 // 2][:, P * (t0 % 2):P * (t1 - t0 + t0 % 2)].bitcast(FP8X4),
                scales=scales[which, e, t0 // 2][:, P * (t0 % 2):P * (t1 - t0 + t0 % 2)],
                in_=grouped[which, e][:, t0:t1].rearrange("p t m j -> p (t m j)"),
            )

        hb = [sb(f"hb{e}", [P, C, PACK], BF16) for e in range(E)]
        hc = {(1, 0, C): sb("hc1", [P, C], U32)}
        hs = {(1, 0, C): sb("hs1", [P, C], U8)}
        for b in range(2):
            hc[0, b * BLK, (b + 1) * BLK] = sb(f"hc0{b}", [P, BLK], U32)
            hs[0, b * BLK, (b + 1) * BLK] = sb(f"hs0{b}", [P, BLK], U8)
        acc1 = {}

        def layer1(e, b, u):
            cols = slice(e * C + b * BLK, e * C + (b + 1) * BLK)
            if (e, b) not in acc1:
                acc1[e, b] = psum.tile([P, PACK, BLK], F32, name=f"acc1_{e}{b}")
            acc = acc1[e, b]
            for t in (2 * u, 2 * u + 1):
                nc.tensor.matmul_mx(
                    out=acc[:, t, :],
                    lhsT=wpw[:, e, 2 * P * t:2 * P * (t + 1)].bitcast(FP4X4),
                    lhsT_scale=wps[e][:, P * t:P * (t + 1)],
                    rhs=gw[1][:, cols].bitcast(FP8X4),
                    rhs_scale=gs[1, e][:, b * BLK:(b + 1) * BLK],
                    start=True,
                    stop=False,
                )
                nc.tensor.matmul_mx(
                    out=acc[:, t, :],
                    lhsT=codes["a", e, t // 2][:, P * (t % 2):P * (t % 2 + 1)].bitcast(FP8X4),
                    lhsT_scale=scales["a", e, t // 2][:, P * (t % 2):P * (t % 2 + 1)],
                    rhs=gw[0][:, cols].bitcast(FP8X4),
                    rhs_scale=gs[0, e][:, b * BLK:(b + 1) * BLK],
                    start=False,
                    stop=True,
                )

        def gelu(e, b):
            nc.scalar.activation(hb[e][:, b * BLK:(b + 1) * BLK, :], acc1[e, b][:].rearrange("p t s -> p s t"), GELU)

        def quant_h(e, s0, s1):
            nc.vector.quantize_mx(
                out=hc[e, s0, s1][:].bitcast(FP8X4),
                scales=hs[e, s0, s1][:],
                in_=hb[e][:, s0:s1, :].rearrange("p s t -> p (s t)"),
            )

        yc = sb("yc", [P, E * C], U32)
        ysc = sb("ysc", [P, E * C], U8)
        y = [sb(f"y{e}", [P, PACK, C], F32) for e in range(E)]
        yb = {(0, 0, C): sb("yb0", [P, C, PACK], BF16)}
        for b in range(2):
            yb[1, b * BLK, (b + 1) * BLK] = sb(f"yb1{b}", [P, BLK, PACK], BF16)
        out_rows = out_0.rearrange("(p t) s -> p t s", t=PACK)
        out_words = out_1[0].rearrange("p s d -> p (s d)").bitcast(I32)
        acc2 = {}

        def pass2(e, t, out, s0, s1):
            nc.tensor.matmul_mx(
                out=out,
                lhsT=codes["b", e, t // 2][:, P * (t % 2):P * (t % 2 + 1)].bitcast(FP8X4),
                lhsT_scale=scales["b", e, t // 2][:, P * (t % 2):P * (t % 2 + 1)],
                rhs=hc[e, s0, s1][:].bitcast(FP8X4),
                rhs_scale=hs[e, s0, s1][:],
                start=True,
                stop=True,
            )

        def layer2_rows(e, t0, t1, bank):
            acc = psum.tile([P, t1 - t0, C], F32, name=bank)
            for t in range(t0, t1):
                for he, s0, s1 in hc:
                    if he == e:
                        pass2(e, t, acc[:, t - t0, s0:s1], s0, s1)
            return acc

        def round_y(e, s0, s1, copy):
            lo, hi = [(a, b) for ye, a, b in yb if ye == e and a <= s0 < b][0]
            copy(
                yb[e, lo, hi][:, s0 - lo:s1 - lo].rearrange("p (c i) t -> p c t i", i=4),
                y[e][:, :, s0:s1].rearrange("p t (c i) -> p c t i", i=4),
            )

        def quant_y(e, s0, s1):
            cols = slice(e * C + s0, e * C + s1)
            nc.vector.quantize_mx(
                out=yc[:, cols].bitcast(FP8X4), scales=ysc[:, cols], in_=yb[e, s0, s1][:].rearrange("p s t -> p (s t)")
            )

        def warm_pe(n, words, plane, m):
            idle = psum.tile([P, E * C], F32, name="acc2_2")
            for i in range(n):
                nc.tensor.matmul_mx(
                    out=idle[0:m, :],
                    lhsT=words[:, 0:m].bitcast(FP8X4),
                    lhsT_scale=plane[:, 0:m],
                    rhs=gw[0][:].bitcast(FP8X4),
                    rhs_scale=gs0[:],
                    start=True,
                    stop=True,
                )

        def store_words(s0, s1):
            nc.sync.dma_start(out_words[:, s0:s1], yc[:, s0:s1].bitcast(I32))

        s_copy = nc.scalar.copy
        v_copy = nc.vector.tensor_copy

        gather_words(0, 0, E * C)
        gather_scales(gs0[:], 0, 0, E * C)
        warm_pe(3, gw[0], gs0, P // 4)
        gather_words(1, 0, E * C)
        gather_scales(gs1[:], 1, 0, E * C)
        deal_scale_bytes(0)
        deal_words()
        cast_w1(0, 0, 2, s_copy)
        cast_w1(0, 2, 4, s_copy)
        quant_w("a", 0, 0, 2)
        quant_w("a", 0, 2, 4)
        deal_scale_pairs(1)
        cast_w1(1, 0, 2, s_copy)
        cast_w1(1, 2, 3, v_copy)
        cast_w1(1, 3, 4, v_copy)
        quant_w("a", 1, 2, 3)
        quant_w("a", 1, 3, 4)
        quant_w("a", 1, 0, 2)
        for e in range(E):
            for b in range(2):
                layer1(e, b, e)
            for b in range(2):
                layer1(e, b, 1 - e)
                gelu(e, b)
        quant_h(0, 0, BLK)
        cast_w2(0, 0, 2, v_copy)
        cast_w2(0, 2, 4, v_copy)
        quant_w("b", 0, 0, 2)
        warm_pe(1, codes["b", 0, 0], scales["b", 0, 0], P // 4)
        quant_h(0, BLK, C)
        quant_w("b", 0, 2, 4)
        quant_h(1, 0, C)
        cast_last(0, 0, 2, s_copy)
        cast_last(0, 2, 4, s_copy)
        cast_last(1, 0, 2, v_copy)
        cast_last(1, 2, 4, v_copy)
        quant_w("b", 1, 0, 1)
        quant_w("b", 1, 1, 2)
        quant_w("b", 1, 2, 4)
        for u in (0, 1):
            s_copy(y[0][:, 2 * u:2 * u + 2, :], layer2_rows(0, 2 * u, 2 * u + 2, f"acc2_0{u}")[:])
            nc.sync.dma_start(out_rows[:, 2 * u:2 * u + 2, 0:C], y[0][:, 2 * u:2 * u + 2, :])
        round_y(0, 0, C, v_copy)
        s_copy(y[1][:, 0:1, :], layer2_rows(1, 0, 1, "acc2_1")[:])
        s_copy(y[1][:, 1:2, :], layer2_rows(1, 1, 2, "acc1_01")[:])
        nc.sync.dma_start(out_rows[:, 0:2, C:2 * C], y[1][:, 0:2, :])
        v_copy(y[1][:, 2:3, :], layer2_rows(1, 2, 3, "acc2_2")[:])
        s_copy(y[1][:, 3:4, :], layer2_rows(1, 3, 4, "acc1_00")[:])
        nc.sync.dma_start(out_rows[:, 2:4, C:2 * C], y[1][:, 2:4, :])
        quant_y(0, 0, C)
        round_y(1, 0, BLK, v_copy)
        round_y(1, BLK, BLK + BLK // 2, v_copy)
        round_y(1, BLK + BLK // 2, C, s_copy)
        quant_y(1, 0, BLK)
        store_words(0, C + BLK)
        quant_y(1, BLK, C)
        store_words(C + BLK, 2 * C)
        for q in range(4):
            nc.sync.dma_start(out_2[0, 4 * q:4 * q + 4, :].bitcast(I32), ysc[32 * q:32 * q + 4, :].bitcast(I32))
